import numpy as np
import ml_dtypes


def mxq(x, axis, fmt="e4m3"):
    dtype, down = {"e4m3": (ml_dtypes.float8_e4m3fn, 7), "e5m2": (ml_dtypes.float8_e5m2, 14)}[fmt]
    v = np.moveaxis(np.asarray(x, np.float32).astype(ml_dtypes.bfloat16).astype(np.float64), axis, -1)
    blocks = v.reshape(v.shape[:-1] + (-1, 32))
    amax = np.abs(blocks).max(-1, keepdims=True)
    byte = np.maximum(np.where(amax > 0, np.frexp(amax)[1] - 1 + 127, 0) - down, 1)
    scale = np.exp2(byte - 127.0)
    codes = (blocks / scale).astype(np.float32).astype(dtype).astype(np.float64)
    return np.moveaxis((codes * scale).reshape(v.shape), -1, axis)


WIDE = False


def mx_kscale(k):
    if not WIDE:
        return np.ones(k)
    levels = np.array([10, -10, 5, -5, 0])
    if k % 512:
        return np.exp2(np.random.permutation(np.resize(levels, k // 32))).repeat(32)
    a = np.empty((k // 512, 16))
    for p in range(k // 512):
        a[p, :8] = np.random.permutation(np.resize(levels, 8))
        for g in range(8):
            far = levels[np.abs(levels - a[p, g]) >= 10]
            a[p, g + 8] = far[np.random.randint(len(far))]
    return np.exp2(a.ravel()).repeat(32)


def f64(x):
    return np.asarray(x).astype(np.float64)


def striped(idx):
    return np.tile(idx.reshape(-1, 16).T, (8, 1)).astype(np.uint16)


def unstriped(offs):
    return offs[:16].T.reshape(-1).astype(np.int64)


E2M1 = np.array([0.0, 0.5, 1.0, 1.5, 2.0, 3.0, 4.0, 6.0, -0.0, -0.5, -1.0, -1.5, -2.0, -3.0, -4.0, -6.0])


def pack_weight(w, fmt):
    k, n = w.shape
    w = f64(np.asarray(w, np.float32).astype(ml_dtypes.bfloat16)).reshape(k // 32, 32, n)
    amax = np.abs(w).max(1)
    if fmt == "e4m3":
        byte = np.frexp(amax)[1] - 1 + 127 - 7
    else:
        mant, ex = np.frexp(amax / 6.0)
        byte = np.where(mant > 0.5, ex, ex - 1) + 127
    byte = np.clip(np.where(amax > 0, byte, 1), 1, 254)
    scaled = (w * np.exp2(127.0 - byte)[:, None, :]).reshape(k, n).astype(np.float32)
    by_word = np.ascontiguousarray(scaled.reshape(k // 512, 128, 4, n).transpose(0, 1, 3, 2))
    if fmt == "e4m3":
        words = by_word.astype(ml_dtypes.float8_e4m3fn).view(np.uint8)
    else:
        c = by_word.astype(ml_dtypes.float4_e2m1fn).view(np.uint8) & 0xF
        words = (c[..., 0::2] | (c[..., 1::2] << 4)).reshape(k // 512, 128, 2 * n)
    return np.ascontiguousarray(words), np.ascontiguousarray(byte.astype(np.uint8).reshape(k // 512, 16, n))


def unpack_weight(words, scales, fmt):
    g, _, n = scales.shape
    words = np.ascontiguousarray(words).reshape(g, 128, n, -1)
    if fmt == "e4m3":
        vals = words.view(ml_dtypes.float8_e4m3fn).astype(np.float64)
    else:
        nib = np.empty((g, 128, n, 4), np.uint8)
        nib[..., 0::2] = words & 0xF
        nib[..., 1::2] = words >> 4
        vals = E2M1[nib]
    vals = vals * np.repeat(np.exp2(scales.astype(np.float64) - 127.0), 8, axis=1)[..., None]
    return vals.transpose(0, 1, 3, 2).reshape(g * 512, n)


def gelu(v):
    return 0.5 * v * (1.0 + np.tanh(np.sqrt(2.0 / np.pi) * (v + 0.044715 * v**3)))


K, KA, T, S, H, T2, P, T3, S2 = 1024, 512, 4096, 1024, 1024, 2048, 512, 2048, 1024

def setup_inputs():
    n = np.random.standard_normal
    s = mx_kscale(K)[:, None]
    u = mx_kscale(H)[:, None]
    tab_words, tab_scales = pack_weight(n((K, T)) * s, "e4m3")
    tab2_words, tab2_scales = pack_weight(n((H, T3)) / u / np.sqrt(H), "e4m3")
    w4_words, w4_scales = pack_weight(n((KA, H)) / s[:KA] / np.sqrt(K), "e2m1")
    return {
        "tab_words": tab_words, "tab_scales": tab_scales,
        "tab2_words": tab2_words, "tab2_scales": tab2_scales,
        "w4_words": w4_words, "w4_scales": w4_scales,
        "w1": (n((K - KA, H)) / s[KA:] / np.sqrt(K)).astype(np.float32),
        "gain": (np.exp(0.4 * n(H)) * u[:, 0]).astype(np.float32),
        "page0": (n((H, T2)) * u).astype(np.float32),
        "wgs": np.exp(0.3 * n((128, S))).astype(np.float32),
        "av": (np.exp(0.4 * n(H)) / u[:, 0]).astype(np.float32),
        "bv": (0.8 * n(S2)).astype(np.float32),
        "offs": striped(np.random.permutation(T)[:S]),
        "offs2": striped(np.random.permutation(T3)[:S2]),
        "offs3": striped(np.random.permutation(T2)[:S]),
        "offs4": striped(np.random.permutation(T2)[:P]),
    }

def reference(tab_words, tab_scales, tab2_words, tab2_scales, w4_words, w4_scales,
              w1, gain, page0, wgs, av, bv, offs, offs2, offs3, offs4):
    v = unpack_weight(tab_words, tab_scales, "e4m3")[:, unstriped(offs)]
    v2 = unpack_weight(tab2_words, tab2_scales, "e4m3")[:, unstriped(offs2)]
    w4 = unpack_weight(w4_words, w4_scales, "e2m1")
    w1q = mxq(f64(w1), 0, "e4m3")
    h = f64(gain)[:, None] * (w4.T @ v[:KA] + w1q.T @ v[KA:])
    page = f64(page0).copy()
    page[:, unstriped(offs3)] = np.tile(f64(wgs), (H // 128, 1)) * h
    x = page[:, unstriped(offs4)]
    z = x * np.tanh(f64(av)[:, None] * x)
    e = v2.T @ mxq(z, 0, "e4m3")
    return e * np.tanh(e + f64(bv)[:, None])

@@ -1,0 +1,279 @@
+from contextlib import ExitStack
+
+import concourse.mybir as mybir
+
+K, KA, T, S, H, T2, NREQ, T3, S2 = 1024, 512, 4096, 1024, 1024, 2048, 512, 2048, 1024
+FLOPS = 2 * K * H * S + 2 * H * S2 * NREQ
+
+F32 = mybir.dt.float32
+BF16 = mybir.dt.bfloat16
+I32 = mybir.dt.int32
+U32 = mybir.dt.uint32
+U16 = mybir.dt.uint16
+U8 = mybir.dt.uint8
+FP8X4 = mybir.dt.float8_e4m3fn_x4
+FP4X4 = mybir.dt.float4_e2m1fn_x4
+MULT = mybir.AluOpType.mult
+COPY = mybir.ActivationFunctionType.Copy
+TANH = mybir.ActivationFunctionType.Tanh
+
+P = 128
+PACK = 4
+PASSES = 2
+BANK = 512
+HALF = NREQ // 2
+H_SLOTS = 4
+PAGE_SLOTS = 5
+BANKS = 8
+
+
+def tile_list_lender_request_scores_kernel(
+    tc, tab_words, tab_scales, tab2_words, tab2_scales, w4_words, w4_scales,
+    w1, gain, page0, wgs, av, bv, offs, offs2, offs3, offs4, out,
+):
+    nc = tc.nc
+    with ExitStack() as ctx:
+        keep = ctx.enter_context(tc.tile_pool(name="keep", bufs=1))
+        psum = ctx.enter_context(tc.psum_pool(name="psum", bufs=1))
+
+        def held(name, shape, dtype, tag=None):
+            return keep.tile(shape, dtype, name=name, tag=tag or name, align_bytes=64)
+
+        def bank(name, b):
+            return psum.tile([P, BANK], F32, name=name, tag="bank%d" % b)
+
+        lists = {}
+
+        def load_list(name, src):
+            lists[name] = keep.tile(list(src.shape), U16, name=name, tag=name)
+            nc.sync.dma_start(lists[name][:], src)
+
+        def load_words(name, src, a):
+            words = held(name, [P, src.shape[2]], U32)
+            nc.sync.dma_start(words[:].bitcast(I32), src[a].rearrange("p t i -> p (t i)").bitcast(I32))
+            return words
+
+        def zeroed_plane(name, width):
+            plane = held(name, [P, width], U8)
+            nc.vector.memset(plane[:].bitcast(I32), 0)
+            return plane
+
+        def load_plane(plane, src):
+            rows = 4 * src.shape[0]
+            for q in range(4):
+                nc.scalar.dma_start(
+                    plane[32 * q : 32 * q + rows, :].bitcast(I32), src[:, 4 * q : 4 * q + 4, :].bitcast(I32)
+                )
+
+        def gather(dst, window, offsets):
+            nc.vector.tensor_copy(dst, window[:].indirect(offsets))
+
+        page_rows = page0.rearrange("(a p t) c -> a t p c", a=PASSES, t=PACK)
+        wgs_rows = wgs.rearrange("(q t) j -> q t j", t=PACK)
+        w1_rows = w1.rearrange("(p j) c -> p j c", j=PACK)
+
+        def load_page(i):
+            page = held("page%d" % i, [P, T2], F32, tag="page%d" % (i % PAGE_SLOTS))
+            nc.sync.dma_start(page[:], page_rows[i // PACK, i % PACK])
+            return page
+
+        def load_wgs(name, t0, t1):
+            dealt = held(name, [P, t1 - t0, S], F32)
+            for q in (0, 2, 1, 3):
+                nc.sync.dma_start(dealt[32 * q : 32 * q + 32, :, :], wgs_rows[:, t0:t1, :])
+            return dealt
+
+        def load_w1(a):
+            raw = held("w1_raw%d" % a, [P, PACK, BANK], F32)
+            nc.sync.dma_start(raw[:], w1_rows[:, :, a * BANK : (a + 1) * BANK])
+            return raw
+
+        w4_plane = zeroed_plane("w4_plane", H)
+        tab_plane = zeroed_plane("tab_plane", T)
+        tab2_plane = zeroed_plane("tab2_plane", T3)
+        w4_raw = held("w4_raw", [P, 2 * H], U8)
+        nc.scalar.dma_start(w4_raw[:].bitcast(I32), w4_words[0].bitcast(I32))
+        tab_tiles = [load_words("tab0", tab_words, 0)]
+        load_list("offs", offs)
+        load_list("offs2", offs2)
+        load_plane(w4_plane, w4_scales)
+        load_plane(tab_plane, tab_scales)
+        load_plane(tab2_plane, tab2_scales)
+        w1_raw = [load_w1(0)]
+        tab_tiles.append(load_words("tab1", tab_words, 1))
+        gain_sb = held("gain", [P, PASSES, PACK], F32)
+        nc.sync.dma_start(gain_sb[:], gain.rearrange("(a p t) -> p a t", a=PASSES, t=PACK))
+        load_list("offs3", offs3)
+        pages = [load_page(0)]
+        wgs_first = load_wgs("wgs_first", 0, 1)
+        load_list("offs4", offs4)
+        av_sb = held("av", [P, PASSES, PACK], F32)
+        nc.sync.dma_start(av_sb[:], av.rearrange("(a p t) -> p a t", a=PASSES, t=PACK))
+        pages.append(load_page(1))
+        wgs_rest = load_wgs("wgs_rest", 1, PACK)
+        w1_raw.append(load_w1(1))
+        pages.append(load_page(2))
+        tab2_tiles = [load_words("tab2_%d" % a, tab2_words, a) for a in range(PASSES)]
+        pages.append(load_page(3))
+        pages.append(load_page(4))
+        bv_sb = held("bv", [P, S2 // P], F32)
+        with nc.allow_non_contiguous_dma(reason="one bias value a partition"):
+            nc.sync.dma_start(bv_sb[:], bv.rearrange("(i p) -> p i", p=P))
+        wgs_of = [wgs_first[:, 0, :]] + [wgs_rest[:, t, :] for t in range(PACK - 1)]
+
+        w4_codes = held("w4_codes", [P, 2 * H], U8)
+        w4_sc = held("w4_sc", [P, H], U8)
+        for a in range(PASSES):
+            nc.vector.tensor_copy(
+                w4_codes[:, a * 1024 : (a + 1) * 1024].rearrange("p (t m e) -> p t m e", t=PACK, e=2),
+                w4_raw[:, a * 1024 : (a + 1) * 1024].rearrange("p (m t e) -> p t m e", t=PACK, e=2),
+            )
+        nc.vector.tensor_copy(
+            w4_sc[:].rearrange("p (a t m) -> p a t m", a=PASSES, t=PACK),
+            w4_plane[:].rearrange("p (a m t) -> p a t m", a=PASSES, t=PACK),
+        )
+
+        v_words = [held("v_words%d" % a, [P, S], U32) for a in range(PASSES)]
+        v_sc = held("v_sc", [P, S], U8)
+        v2_words = [held("v2_words%d" % a, [P, S2], U32) for a in range(PASSES)]
+        v2_sc = held("v2_sc", [P, S2], U8)
+        w1_codes = [held("w1_codes%d" % a, [P, BANK], U32) for a in range(PASSES)]
+        w1_sc = [held("w1_sc%d" % a, [P, BANK], U8) for a in range(PASSES)]
+
+        def quantise_w1(a):
+            rounded = held("w1_bf%d" % a, [P, BANK * PACK], BF16)
+            nc.scalar.copy(
+                rounded[:].rearrange("p (t m j) -> p m j t", t=PACK, j=PACK),
+                w1_raw[a][:].rearrange("p j (m t) -> p m j t", t=PACK),
+            )
+            nc.vector.quantize_mx(out=w1_codes[a][:].bitcast(FP8X4), scales=w1_sc[a][:], in_=rounded[:])
+
+        gather(v_words[0][:], tab_tiles[0], lists["offs"][:])
+        gather(v_sc[:], tab_plane, lists["offs"][:])
+        quantise_w1(0)
+        gather(v2_sc[:], tab2_plane, lists["offs2"][:])
+        for u in range(2):
+            gather(v_words[1][:, u * BANK : (u + 1) * BANK], tab_tiles[1], lists["offs"][:, 32 * u : 32 * u + 32])
+
+        def first_product(i):
+            a, t = divmod(i, PACK)
+            h = held("h%d" % i, [P, S], F32, tag="h%d" % (i % H_SLOTS))
+            col = slice(i * P, (i + 1) * P)
+            for u in range(2):
+                j = slice(u * BANK, (u + 1) * BANK)
+                acc = bank("h_acc%d_%d" % (i, u), (2 * i + u) % BANKS)
+                nc.tensor.matmul_mx(
+                    out=acc[:], lhsT=w4_codes[:, 2 * i * P : 2 * (i + 1) * P].bitcast(FP4X4),
+                    lhsT_scale=w4_sc[:, col], rhs=v_words[0][:, j].bitcast(FP8X4), rhs_scale=v_sc[:, j],
+                    start=True, stop=False,
+                )
+                nc.tensor.matmul_mx(
+                    out=acc[:], lhsT=w1_codes[a][:, t * P : (t + 1) * P].bitcast(FP8X4),
+                    lhsT_scale=w1_sc[a][:, t * P : (t + 1) * P], rhs=v_words[1][:, j].bitcast(FP8X4),
+                    rhs_scale=v_sc[4:, j], start=False, stop=True,
+                )
+                nc.scalar.activation(h[:, j], acc[:], COPY, scale=gain_sb[:, a, t : t + 1])
+            return h
+
+        def scatter(i, h, pieces):
+            width = S // pieces
+            for u in range(pieces):
+                j = slice(u * width, (u + 1) * width)
+                offsets = lists["offs3"][:, u * width // 16 : (u + 1) * width // 16]
+                nc.vector.tensor_tensor(pages[i][:].indirect(offsets), h[:, j], wgs_of[i % PACK][:, j], MULT)
+
+        def fetch(i, x, th, n0):
+            a, t = divmod(i, PACK)
+            width = x.shape[2]
+            gather(x[:, t, :], pages[i], lists["offs4"][:, n0 // 16 : (n0 + width) // 16])
+            nc.scalar.activation(th[:, t, :], x[:, t, :], TANH, scale=av_sb[:, a, t : t + 1])
+
+        def round_z(name, x, th, tag=None):
+            z = held(name, [P, x.shape[2] * PACK], BF16, tag=tag)
+            nc.vector.tensor_tensor(
+                z[:].rearrange("p (c i t) -> p c t i", i=4, t=PACK),
+                x[:].rearrange("p t (c i) -> p c t i", i=4),
+                th[:].rearrange("p t (c i) -> p c t i", i=4),
+                MULT,
+            )
+            return z
+
+        def quantise_z(name, z, tag=None):
+            width = z.shape[1] // PACK
+            codes = held(name + "_codes", [P, width], U32, tag=tag)
+            sc = held(name + "_sc", [P, width], U8)
+            nc.vector.quantize_mx(out=codes[:].bitcast(FP8X4), scales=sc[:], in_=z[:])
+            return codes, sc
+
+        def second_pass(acc, pair, a, codes, sc):
+            for w in range(2):
+                m = slice((2 * pair + w) * P, (2 * pair + w + 1) * P)
+                nc.tensor.matmul_mx(
+                    out=acc[:, w * HALF : (w + 1) * HALF], lhsT=v2_words[a][:, m].bitcast(FP8X4),
+                    lhsT_scale=v2_sc[4 * a :, m], rhs=codes.bitcast(FP8X4), rhs_scale=sc,
+                    start=(a == 0 and w == 0), stop=(a == PASSES - 1 and w == 1),
+                )
+
+        out_rows = out.rearrange("(i p) n -> p i n", p=P)
+
+        def finish(acc, pair, u):
+            th = held("e_tanh%d_%d" % (u, pair), [P, BANK], F32, tag="e_tanh%d" % pair)
+            for w in range(2):
+                n = slice(w * HALF, (w + 1) * HALF)
+                nc.scalar.activation(th[:, n], acc[:, n], TANH, bias=bv_sb[:, 2 * pair + w : 2 * pair + w + 1])
+            score = held("score%d_%d" % (u, pair), [P, BANK], F32, tag="score%d" % pair)
+            nc.vector.tensor_tensor(score[:], acc[:], th[:], MULT)
+            nc.sync.dma_start(
+                out_rows[:, 2 * pair : 2 * pair + 2, u * HALF : (u + 1) * HALF],
+                score[:].rearrange("p (w n) -> p w n", w=2),
+            )
+
+        hs = [first_product(i) for i in range(H_SLOTS)]
+        quantise_w1(1)
+        x0 = held("x0", [P, PACK, NREQ], F32)
+        th0 = held("th0", [P, PACK, NREQ], F32, tag="w1_raw0")
+        for i in range(PACK):
+            scatter(i, hs[i], 2 if i == 0 else 1)
+            hs.append(first_product(i + H_SLOTS))
+            fetch(i, x0, th0, 0)
+            if i + PAGE_SLOTS < PASSES * PACK:
+                pages.append(load_page(i + PAGE_SLOTS))
+            if i >= 2:
+                gather(v2_words[i - 2][:], tab2_tiles[i - 2], lists["offs2"][:])
+
+        x1 = [held("x1_0", [P, PACK, HALF], F32)]
+        th1 = [held("th1_%d" % u, [P, PACK, HALF], F32) for u in range(2)]
+        scatter(4, hs[4], 1)
+        fetch(4, x1[0], th1[0], 0)
+        z0 = round_z("z0", x0, th0, tag="h0")
+        scatter(5, hs[5], 1)
+        fetch(5, x1[0], th1[0], 0)
+        codes0, sc0 = quantise_z("z0", z0, tag="h1")
+        accs = [[bank("e%d_%d" % (u, pair), 4 * u + pair) for pair in range(4)] for u in range(2)]
+        for u in range(2):
+            for pair in range(4):
+                n = slice(u * HALF, (u + 1) * HALF)
+                second_pass(accs[u][pair], pair, 0, codes0[:, n], sc0[:, n])
+        for i in (6, 7):
+            scatter(i, hs[i], 1)
+            fetch(i, x1[0], th1[0], 0)
+
+        x1.append(held("x1_1", [P, PACK, HALF], F32, tag="h3"))
+        fetch(4, x1[1], th1[1], HALF)
+        z1 = [round_z("z1_0", x1[0], th1[0])]
+        fetch(5, x1[1], th1[1], HALF)
+        codes1, sc1 = quantise_z("z1_0", z1[0])
+        for pair in range(4):
+            second_pass(accs[0][pair], pair, 1, codes1[:], sc1[:])
+        fetch(6, x1[1], th1[1], HALF)
+        fetch(7, x1[1], th1[1], HALF)
+        finish(accs[0][0], 0, 0)
+        z1.append(round_z("z1_1", x1[1], th1[1]))
+        finish(accs[0][1], 1, 0)
+        codes1, sc1 = quantise_z("z1_1", z1[1])
+        for pair in range(4):
+            second_pass(accs[1][pair], pair, 1, codes1[:], sc1[:])
+        finish(accs[0][2], 2, 0)
+        finish(accs[0][3], 3, 0)
+        for pair in range(4):
+            finish(accs[1][pair], pair, 1)

@@ -23,7 +23,6 @@ PASSES = 2
 BANK = 512
 HALF = NREQ // 2
 H_SLOTS = 4
-PAGE_SLOTS = 5
 BANKS = 8
 
 
@@ -53,17 +52,25 @@ def tile_list_lender_request_scores_kernel(
             nc.sync.dma_start(words[:].bitcast(I32), src[a].rearrange("p t i -> p (t i)").bitcast(I32))
             return words
 
-        def zeroed_plane(name, width):
+        def zeroed_plane(engine, name, width):
             plane = held(name, [P, width], U8)
-            nc.vector.memset(plane[:].bitcast(I32), 0)
+            engine.memset(plane[:].bitcast(I32), 0)
             return plane
 
-        def load_plane(plane, src):
-            rows = 4 * src.shape[0]
-            for q in range(4):
-                nc.scalar.dma_start(
-                    plane[32 * q : 32 * q + rows, :].bitcast(I32), src[:, 4 * q : 4 * q + 4, :].bitcast(I32)
+        def load_scale_rows(name, src):
+            rows = held(name, [P, src.shape[2]], U8)
+            nc.vector.memset(rows[32:64, :].bitcast(I32), 0)
+            nc.vector.memset(rows[64:, :].bitcast(I32), 0)
+            for a in range(PASSES):
+                nc.sync.dma_start(
+                    rows[16 * a : 16 * a + 16, :].bitcast(I32),
+                    src[a].rearrange("(q r) n -> r q n", r=4).bitcast(I32),
                 )
+            return rows
+
+        def place_scale_rows(plane, picked):
+            for q in range(4):
+                nc.gpsimd.dma_start(plane[32 * q : 32 * q + 8, :].bitcast(I32), picked[q:32:4, :].bitcast(I32))
 
         def gather(dst, window, offsets):
             nc.vector.tensor_copy(dst, window[:].indirect(offsets))
@@ -73,14 +80,14 @@ def tile_list_lender_request_scores_kernel(
         w1_rows = w1.rearrange("(p j) c -> p j c", j=PACK)
 
         def load_page(i):
-            page = held("page%d" % i, [P, T2], F32, tag="page%d" % (i % PAGE_SLOTS))
+            page = held("page%d" % i, [P, T2], F32)
             nc.sync.dma_start(page[:], page_rows[i // PACK, i % PACK])
             return page
 
-        def load_wgs(name, t0, t1):
-            dealt = held(name, [P, t1 - t0, S], F32)
+        def load_wgs(queue, t):
+            dealt = held("wgs%d" % t, [P, S], F32)
             for q in (0, 2, 1, 3):
-                nc.sync.dma_start(dealt[32 * q : 32 * q + 32, :, :], wgs_rows[:, t0:t1, :])
+                queue.dma_start(dealt[32 * q : 32 * q + 32, :], wgs_rows[:, t, :])
             return dealt
 
         def load_w1(a):
@@ -88,38 +95,41 @@ def tile_list_lender_request_scores_kernel(
             nc.sync.dma_start(raw[:], w1_rows[:, :, a * BANK : (a + 1) * BANK])
             return raw
 
-        w4_plane = zeroed_plane("w4_plane", H)
-        tab_plane = zeroed_plane("tab_plane", T)
-        tab2_plane = zeroed_plane("tab2_plane", T3)
+        load_list("offs", offs)
         w4_raw = held("w4_raw", [P, 2 * H], U8)
         nc.scalar.dma_start(w4_raw[:].bitcast(I32), w4_words[0].bitcast(I32))
+        tab_rows = load_scale_rows("tab_rows", tab_scales)
+        w4_plane = zeroed_plane(nc.vector, "w4_plane", H)
         tab_tiles = [load_words("tab0", tab_words, 0)]
-        load_list("offs", offs)
-        load_list("offs2", offs2)
-        load_plane(w4_plane, w4_scales)
-        load_plane(tab_plane, tab_scales)
-        load_plane(tab2_plane, tab2_scales)
         w1_raw = [load_w1(0)]
+        load_list("offs2", offs2)
+        tab2_rows = load_scale_rows("tab2_rows", tab2_scales)
         tab_tiles.append(load_words("tab1", tab_words, 1))
+        for q in range(4):
+            nc.scalar.dma_start(
+                w4_plane[32 * q : 32 * q + 4, :].bitcast(I32), w4_scales[0, 4 * q : 4 * q + 4, :].bitcast(I32)
+            )
+        v_sc = zeroed_plane(nc.gpsimd, "v_sc", S)
+        v2_sc = zeroed_plane(nc.gpsimd, "v2_sc", S2)
+        wgs_of = [load_wgs(nc.gpsimd, 0)]
         gain_sb = held("gain", [P, PASSES, PACK], F32)
         nc.sync.dma_start(gain_sb[:], gain.rearrange("(a p t) -> p a t", a=PASSES, t=PACK))
         load_list("offs3", offs3)
-        pages = [load_page(0)]
-        wgs_first = load_wgs("wgs_first", 0, 1)
+        pages = [load_page(0), load_page(1)]
+        wgs_of.append(load_wgs(nc.sync, 1))
+        pages.append(load_page(2))
+        wgs_of.append(load_wgs(nc.sync, 2))
+        w1_raw.append(load_w1(1))
+        pages.append(load_page(3))
+        wgs_of.append(load_wgs(nc.sync, 3))
+        tab2_tiles = [load_words("tab2_%d" % a, tab2_words, a) for a in range(PASSES)]
+        pages.extend(load_page(i) for i in range(PACK, PASSES * PACK))
         load_list("offs4", offs4)
         av_sb = held("av", [P, PASSES, PACK], F32)
         nc.sync.dma_start(av_sb[:], av.rearrange("(a p t) -> p a t", a=PASSES, t=PACK))
-        pages.append(load_page(1))
-        wgs_rest = load_wgs("wgs_rest", 1, PACK)
-        w1_raw.append(load_w1(1))
-        pages.append(load_page(2))
-        tab2_tiles = [load_words("tab2_%d" % a, tab2_words, a) for a in range(PASSES)]
-        pages.append(load_page(3))
-        pages.append(load_page(4))
         bv_sb = held("bv", [P, S2 // P], F32)
         with nc.allow_non_contiguous_dma(reason="one bias value a partition"):
             nc.sync.dma_start(bv_sb[:], bv.rearrange("(i p) -> p i", p=P))
-        wgs_of = [wgs_first[:, 0, :]] + [wgs_rest[:, t, :] for t in range(PACK - 1)]
 
         w4_codes = held("w4_codes", [P, 2 * H], U8)
         w4_sc = held("w4_sc", [P, H], U8)
@@ -134,9 +144,9 @@ def tile_list_lender_request_scores_kernel(
         )
 
         v_words = [held("v_words%d" % a, [P, S], U32) for a in range(PASSES)]
-        v_sc = held("v_sc", [P, S], U8)
+        v_picked = held("v_picked", [P, S], U8)
         v2_words = [held("v2_words%d" % a, [P, S2], U32) for a in range(PASSES)]
-        v2_sc = held("v2_sc", [P, S2], U8)
+        v2_picked = held("v2_picked", [P, S2], U8)
         w1_codes = [held("w1_codes%d" % a, [P, BANK], U32) for a in range(PASSES)]
         w1_sc = [held("w1_sc%d" % a, [P, BANK], U8) for a in range(PASSES)]
 
@@ -148,10 +158,12 @@ def tile_list_lender_request_scores_kernel(
             )
             nc.vector.quantize_mx(out=w1_codes[a][:].bitcast(FP8X4), scales=w1_sc[a][:], in_=rounded[:])
 
+        gather(v_picked[:], tab_rows, lists["offs"][:])
+        place_scale_rows(v_sc, v_picked)
         gather(v_words[0][:], tab_tiles[0], lists["offs"][:])
-        gather(v_sc[:], tab_plane, lists["offs"][:])
         quantise_w1(0)
-        gather(v2_sc[:], tab2_plane, lists["offs2"][:])
+        gather(v2_picked[:], tab2_rows, lists["offs2"][:])
+        place_scale_rows(v2_sc, v2_picked)
         for u in range(2):
             gather(v_words[1][:, u * BANK : (u + 1) * BANK], tab_tiles[1], lists["offs"][:, 32 * u : 32 * u + 32])
 
@@ -192,8 +204,8 @@ def tile_list_lender_request_scores_kernel(
             z = held(name, [P, x.shape[2] * PACK], BF16, tag=tag)
             nc.vector.tensor_tensor(
                 z[:].rearrange("p (c i t) -> p c t i", i=4, t=PACK),
-                x[:].rearrange("p t (c i) -> p c t i", i=4),
-                th[:].rearrange("p t (c i) -> p c t i", i=4),
+                x.rearrange("p t (c i) -> p c t i", i=4),
+                th.rearrange("p t (c i) -> p c t i", i=4),
                 MULT,
             )
             return z
@@ -217,63 +229,47 @@ def tile_list_lender_request_scores_kernel(
         out_rows = out.rearrange("(i p) n -> p i n", p=P)
 
         def finish(acc, pair, u):
-            th = held("e_tanh%d_%d" % (u, pair), [P, BANK], F32, tag="e_tanh%d" % pair)
+            th = e_tanh[:, 4 * u + pair, :]
             for w in range(2):
                 n = slice(w * HALF, (w + 1) * HALF)
                 nc.scalar.activation(th[:, n], acc[:, n], TANH, bias=bv_sb[:, 2 * pair + w : 2 * pair + w + 1])
-            score = held("score%d_%d" % (u, pair), [P, BANK], F32, tag="score%d" % pair)
-            nc.vector.tensor_tensor(score[:], acc[:], th[:], MULT)
+            score = scores[:, 4 * u + pair, :]
+            nc.vector.tensor_tensor(score, acc[:], th, MULT)
             nc.sync.dma_start(
                 out_rows[:, 2 * pair : 2 * pair + 2, u * HALF : (u + 1) * HALF],
-                score[:].rearrange("p (w n) -> p w n", w=2),
+                score.rearrange("p (w n) -> p w n", w=2),
             )
 
         hs = [first_product(i) for i in range(H_SLOTS)]
         quantise_w1(1)
-        x0 = held("x0", [P, PACK, NREQ], F32)
-        th0 = held("th0", [P, PACK, NREQ], F32, tag="w1_raw0")
-        for i in range(PACK):
+        for i in range(PASSES * PACK):
             scatter(i, hs[i], 2 if i == 0 else 1)
-            hs.append(first_product(i + H_SLOTS))
-            fetch(i, x0, th0, 0)
-            if i + PAGE_SLOTS < PASSES * PACK:
-                pages.append(load_page(i + PAGE_SLOTS))
-            if i >= 2:
-                gather(v2_words[i - 2][:], tab2_tiles[i - 2], lists["offs2"][:])
+            if i + H_SLOTS < PASSES * PACK:
+                hs.append(first_product(i + H_SLOTS))
+            if i in (3, 4):
+                gather(v2_words[i - 3][:], tab2_tiles[i - 3], lists["offs2"][:])
 
-        x1 = [held("x1_0", [P, PACK, HALF], F32)]
-        th1 = [held("th1_%d" % u, [P, PACK, HALF], F32) for u in range(2)]
-        scatter(4, hs[4], 1)
-        fetch(4, x1[0], th1[0], 0)
-        z0 = round_z("z0", x0, th0, tag="h0")
-        scatter(5, hs[5], 1)
-        fetch(5, x1[0], th1[0], 0)
-        codes0, sc0 = quantise_z("z0", z0, tag="h1")
+        x_all = held("x_all", [P, PASSES, PACK, HALF], F32, tag="wgs3")
+        e_tanh = held("e_tanh", [P, BANKS, BANK], F32, tag="tab0")
+        scores = held("scores", [P, BANKS, BANK], F32, tag="tab1")
+        th_all = held("th_all", [P, PASSES, PACK, HALF], F32, tag="w1_raw0")
         accs = [[bank("e%d_%d" % (u, pair), 4 * u + pair) for pair in range(4)] for u in range(2)]
+
+        def fetch_pass(a, u):
+            for i in range(a * PACK, (a + 1) * PACK):
+                fetch(i, x_all[:, a, :, :], th_all[:, a, :, :], u * HALF)
+
+        def multiply(a, u, z):
+            codes, sc = quantise_z("z%d_%d" % (a, u), z)
+            for pair in range(4):
+                second_pass(accs[u][pair], pair, a, codes[:], sc[:])
+
+        for u in range(2):
+            for a in range(PASSES):
+                fetch_pass(a, u)
+            zs = [round_z("z%d_%d" % (a, u), x_all[:, a, :, :], th_all[:, a, :, :]) for a in range(PASSES)]
+            for a in range(PASSES):
+                multiply(a, u, zs[a])
         for u in range(2):
             for pair in range(4):
-                n = slice(u * HALF, (u + 1) * HALF)
-                second_pass(accs[u][pair], pair, 0, codes0[:, n], sc0[:, n])
-        for i in (6, 7):
-            scatter(i, hs[i], 1)
-            fetch(i, x1[0], th1[0], 0)
-
-        x1.append(held("x1_1", [P, PACK, HALF], F32, tag="h3"))
-        fetch(4, x1[1], th1[1], HALF)
-        z1 = [round_z("z1_0", x1[0], th1[0])]
-        fetch(5, x1[1], th1[1], HALF)
-        codes1, sc1 = quantise_z("z1_0", z1[0])
-        for pair in range(4):
-            second_pass(accs[0][pair], pair, 1, codes1[:], sc1[:])
-        fetch(6, x1[1], th1[1], HALF)
-        fetch(7, x1[1], th1[1], HALF)
-        finish(accs[0][0], 0, 0)
-        z1.append(round_z("z1_1", x1[1], th1[1]))
-        finish(accs[0][1], 1, 0)
-        codes1, sc1 = quantise_z("z1_1", z1[1])
-        for pair in range(4):
-            second_pass(accs[1][pair], pair, 1, codes1[:], sc1[:])
-        finish(accs[0][2], 2, 0)
-        finish(accs[0][3], 3, 0)
-        for pair in range(4):
-            finish(accs[1][pair], pair, 1)
+                finish(accs[u][pair], pair, u)

@@ -210,6 +210,15 @@ def tile_list_lender_request_scores_kernel(
             )
             return z
 
+        def round_z_aside(name, x, th):
+            planes = held(name + "_planes", [P, PACK, x.shape[2]], BF16)
+            nc.gpsimd.tensor_tensor(planes[:], x, th, MULT)
+            z = held(name, [P, x.shape[2] * PACK], BF16)
+            nc.scalar.copy(
+                z[:].rearrange("p (c i t) -> p c t i", i=4, t=PACK), planes[:].rearrange("p t (c i) -> p c t i", i=4)
+            )
+            return z
+
         def quantise_z(name, z, tag=None):
             width = z.shape[1] // PACK
             codes = held(name + "_codes", [P, width], U32, tag=tag)
@@ -249,7 +258,7 @@ def tile_list_lender_request_scores_kernel(
             if i in (3, 4):
                 gather(v2_words[i - 3][:], tab2_tiles[i - 3], lists["offs2"][:])
 
-        x_all = held("x_all", [P, PASSES, PACK, HALF], F32, tag="wgs3")
+        x_all = held("x_all", [P, PASSES, PACK, HALF], F32, tag="h3")
         e_tanh = held("e_tanh", [P, BANKS, BANK], F32, tag="tab0")
         scores = held("scores", [P, BANKS, BANK], F32, tag="tab1")
         th_all = held("th_all", [P, PASSES, PACK, HALF], F32, tag="w1_raw0")
@@ -267,7 +276,10 @@ def tile_list_lender_request_scores_kernel(
         for u in range(2):
             for a in range(PASSES):
                 fetch_pass(a, u)
-            zs = [round_z("z%d_%d" % (a, u), x_all[:, a, :, :], th_all[:, a, :, :]) for a in range(PASSES)]
+            zs = [
+                rounder("z%d_%d" % (a, u), x_all[:, a, :, :], th_all[:, a, :, :])
+                for a, rounder in enumerate((round_z_aside, round_z if u == 1 else round_z_aside))
+            ]
             for a in range(PASSES):
                 multiply(a, u, zs[a])
         for u in range(2):

from contextlib import ExitStack

import concourse.mybir as mybir

K, KA, T, S, H, T2, NREQ, T3, S2 = 1024, 512, 4096, 1024, 1024, 2048, 512, 2048, 1024
FLOPS = 2 * K * H * S + 2 * H * S2 * NREQ

F32 = mybir.dt.float32
BF16 = mybir.dt.bfloat16
I32 = mybir.dt.int32
U32 = mybir.dt.uint32
U16 = mybir.dt.uint16
U8 = mybir.dt.uint8
FP8X4 = mybir.dt.float8_e4m3fn_x4
FP4X4 = mybir.dt.float4_e2m1fn_x4
MULT = mybir.AluOpType.mult
COPY = mybir.ActivationFunctionType.Copy
TANH = mybir.ActivationFunctionType.Tanh

P = 128
PACK = 4
PASSES = 2
BANK = 512
HALF = NREQ // 2
H_SLOTS = 4
BANKS = 8


def tile_list_lender_request_scores_kernel(
    tc, tab_words, tab_scales, tab2_words, tab2_scales, w4_words, w4_scales,
    w1, gain, page0, wgs, av, bv, offs, offs2, offs3, offs4, out,
):
    nc = tc.nc
    with ExitStack() as ctx:
        keep = ctx.enter_context(tc.tile_pool(name="keep", bufs=1))
        psum = ctx.enter_context(tc.psum_pool(name="psum", bufs=1))

        def held(name, shape, dtype, tag=None):
            return keep.tile(shape, dtype, name=name, tag=tag or name, align_bytes=64)

        def bank(name, b):
            return psum.tile([P, BANK], F32, name=name, tag="bank%d" % b)

        lists = {}

        def load_list(name, src):
            lists[name] = keep.tile(list(src.shape), U16, name=name, tag=name)
            nc.sync.dma_start(lists[name][:], src)

        def load_words(name, src, a):
            words = held(name, [P, src.shape[2]], U32)
            nc.sync.dma_start(words[:].bitcast(I32), src[a].rearrange("p t i -> p (t i)").bitcast(I32))
            return words

        def zeroed_plane(engine, name, width):
            plane = held(name, [P, width], U8)
            engine.memset(plane[:].bitcast(I32), 0)
            return plane

        def load_scale_rows(name, src):
            rows = held(name, [P, src.shape[2]], U8)
            nc.vector.memset(rows[32:64, :].bitcast(I32), 0)
            nc.vector.memset(rows[64:, :].bitcast(I32), 0)
            for a in range(PASSES):
                nc.sync.dma_start(
                    rows[16 * a : 16 * a + 16, :].bitcast(I32),
                    src[a].rearrange("(q r) n -> r q n", r=4).bitcast(I32),
                )
            return rows

        def place_scale_rows(plane, picked):
            for q in range(4):
                nc.gpsimd.dma_start(plane[32 * q : 32 * q + 8, :].bitcast(I32), picked[q:32:4, :].bitcast(I32))

        def gather(dst, window, offsets):
            nc.vector.tensor_copy(dst, window[:].indirect(offsets))

        page_rows = page0.rearrange("(a p t) c -> a t p c", a=PASSES, t=PACK)
        wgs_rows = wgs.rearrange("(q t) j -> q t j", t=PACK)
        w1_rows = w1.rearrange("(p j) c -> p j c", j=PACK)

        def load_page(i):
            page = held("page%d" % i, [P, T2], F32)
            nc.sync.dma_start(page[:], page_rows[i // PACK, i % PACK])
            return page

        def load_wgs(queue, t):
            dealt = held("wgs%d" % t, [P, S], F32)
            for q in (0, 2, 1, 3):
                queue.dma_start(dealt[32 * q : 32 * q + 32, :], wgs_rows[:, t, :])
            return dealt

        def load_w1(a):
            raw = held("w1_raw%d" % a, [P, PACK, BANK], F32)
            nc.sync.dma_start(raw[:], w1_rows[:, :, a * BANK : (a + 1) * BANK])
            return raw

        load_list("offs", offs)
        w4_raw = held("w4_raw", [P, 2 * H], U8)
        nc.scalar.dma_start(w4_raw[:].bitcast(I32), w4_words[0].bitcast(I32))
        tab_rows = load_scale_rows("tab_rows", tab_scales)
        w4_plane = zeroed_plane(nc.vector, "w4_plane", H)
        tab_tiles = [load_words("tab0", tab_words, 0)]
        w1_raw = [load_w1(0)]
        load_list("offs2", offs2)
        tab2_rows = load_scale_rows("tab2_rows", tab2_scales)
        tab_tiles.append(load_words("tab1", tab_words, 1))
        for q in range(4):
            nc.scalar.dma_start(
                w4_plane[32 * q : 32 * q + 4, :].bitcast(I32), w4_scales[0, 4 * q : 4 * q + 4, :].bitcast(I32)
            )
        v_sc = zeroed_plane(nc.gpsimd, "v_sc", S)
        v2_sc = zeroed_plane(nc.gpsimd, "v2_sc", S2)
        wgs_of = [load_wgs(nc.gpsimd, 0)]
        gain_sb = held("gain", [P, PASSES, PACK], F32)
        nc.sync.dma_start(gain_sb[:], gain.rearrange("(a p t) -> p a t", a=PASSES, t=PACK))
        load_list("offs3", offs3)
        pages = [load_page(0), load_page(1)]
        wgs_of.append(load_wgs(nc.sync, 1))
        pages.append(load_page(2))
        wgs_of.append(load_wgs(nc.sync, 2))
        w1_raw.append(load_w1(1))
        pages.append(load_page(3))
        wgs_of.append(load_wgs(nc.sync, 3))
        tab2_tiles = [load_words("tab2_%d" % a, tab2_words, a) for a in range(PASSES)]
        pages.extend(load_page(i) for i in range(PACK, PASSES * PACK))
        load_list("offs4", offs4)
        av_sb = held("av", [P, PASSES, PACK], F32)
        nc.sync.dma_start(av_sb[:], av.rearrange("(a p t) -> p a t", a=PASSES, t=PACK))
        bv_sb = held("bv", [P, S2 // P], F32)
        with nc.allow_non_contiguous_dma(reason="one bias value a partition"):
            nc.sync.dma_start(bv_sb[:], bv.rearrange("(i p) -> p i", p=P))

        w4_codes = held("w4_codes", [P, 2 * H], U8)
        w4_sc = held("w4_sc", [P, H], U8)
        for a in range(PASSES):
            nc.vector.tensor_copy(
                w4_codes[:, a * 1024 : (a + 1) * 1024].rearrange("p (t m e) -> p t m e", t=PACK, e=2),
                w4_raw[:, a * 1024 : (a + 1) * 1024].rearrange("p (m t e) -> p t m e", t=PACK, e=2),
            )
        nc.vector.tensor_copy(
            w4_sc[:].rearrange("p (a t m) -> p a t m", a=PASSES, t=PACK),
            w4_plane[:].rearrange("p (a m t) -> p a t m", a=PASSES, t=PACK),
        )

        v_words = [held("v_words%d" % a, [P, S], U32) for a in range(PASSES)]
        v_picked = held("v_picked", [P, S], U8)
        v2_words = [held("v2_words%d" % a, [P, S2], U32) for a in range(PASSES)]
        v2_picked = held("v2_picked", [P, S2], U8)
        w1_codes = [held("w1_codes%d" % a, [P, BANK], U32) for a in range(PASSES)]
        w1_sc = [held("w1_sc%d" % a, [P, BANK], U8) for a in range(PASSES)]

        def quantise_w1(a):
            rounded = held("w1_bf%d" % a, [P, BANK * PACK], BF16)
            nc.scalar.copy(
                rounded[:].rearrange("p (t m j) -> p m j t", t=PACK, j=PACK),
                w1_raw[a][:].rearrange("p j (m t) -> p m j t", t=PACK),
            )
            nc.vector.quantize_mx(out=w1_codes[a][:].bitcast(FP8X4), scales=w1_sc[a][:], in_=rounded[:])

        gather(v_picked[:], tab_rows, lists["offs"][:])
        place_scale_rows(v_sc, v_picked)
        gather(v_words[0][:], tab_tiles[0], lists["offs"][:])
        quantise_w1(0)
        gather(v2_picked[:], tab2_rows, lists["offs2"][:])
        place_scale_rows(v2_sc, v2_picked)
        for u in range(2):
            gather(v_words[1][:, u * BANK : (u + 1) * BANK], tab_tiles[1], lists["offs"][:, 32 * u : 32 * u + 32])

        def first_product(i):
            a, t = divmod(i, PACK)
            h = held("h%d" % i, [P, S], F32, tag="h%d" % (i % H_SLOTS))
            col = slice(i * P, (i + 1) * P)
            for u in range(2):
                j = slice(u * BANK, (u + 1) * BANK)
                acc = bank("h_acc%d_%d" % (i, u), (2 * i + u) % BANKS)
                nc.tensor.matmul_mx(
                    out=acc[:], lhsT=w4_codes[:, 2 * i * P : 2 * (i + 1) * P].bitcast(FP4X4),
                    lhsT_scale=w4_sc[:, col], rhs=v_words[0][:, j].bitcast(FP8X4), rhs_scale=v_sc[:, j],
                    start=True, stop=False,
                )
                nc.tensor.matmul_mx(
                    out=acc[:], lhsT=w1_codes[a][:, t * P : (t + 1) * P].bitcast(FP8X4),
                    lhsT_scale=w1_sc[a][:, t * P : (t + 1) * P], rhs=v_words[1][:, j].bitcast(FP8X4),
                    rhs_scale=v_sc[4:, j], start=False, stop=True,
                )
                nc.scalar.activation(h[:, j], acc[:], COPY, scale=gain_sb[:, a, t : t + 1])
            return h

        def scatter(i, h, pieces):
            width = S // pieces
            for u in range(pieces):
                j = slice(u * width, (u + 1) * width)
                offsets = lists["offs3"][:, u * width // 16 : (u + 1) * width // 16]
                nc.vector.tensor_tensor(pages[i][:].indirect(offsets), h[:, j], wgs_of[i % PACK][:, j], MULT)

        def fetch(i, x, th, n0):
            a, t = divmod(i, PACK)
            width = x.shape[2]
            gather(x[:, t, :], pages[i], lists["offs4"][:, n0 // 16 : (n0 + width) // 16])
            nc.scalar.activation(th[:, t, :], x[:, t, :], TANH, scale=av_sb[:, a, t : t + 1])

        def round_z(name, x, th, tag=None):
            z = held(name, [P, x.shape[2] * PACK], BF16, tag=tag)
            nc.vector.tensor_tensor(
                z[:].rearrange("p (c i t) -> p c t i", i=4, t=PACK),
                x.rearrange("p t (c i) -> p c t i", i=4),
                th.rearrange("p t (c i) -> p c t i", i=4),
                MULT,
            )
            return z

        def round_z_aside(name, x, th):
            planes = held(name + "_planes", [P, PACK, x.shape[2]], BF16)
            nc.gpsimd.tensor_tensor(planes[:], x, th, MULT)
            z = held(name, [P, x.shape[2] * PACK], BF16)
            nc.scalar.copy(
                z[:].rearrange("p (c i t) -> p c t i", i=4, t=PACK), planes[:].rearrange("p t (c i) -> p c t i", i=4)
            )
            return z

        def quantise_z(name, z, tag=None):
            width = z.shape[1] // PACK
            codes = held(name + "_codes", [P, width], U32, tag=tag)
            sc = held(name + "_sc", [P, width], U8)
            nc.vector.quantize_mx(out=codes[:].bitcast(FP8X4), scales=sc[:], in_=z[:])
            return codes, sc

        def second_pass(acc, pair, a, codes, sc):
            for w in range(2):
                m = slice((2 * pair + w) * P, (2 * pair + w + 1) * P)
                nc.tensor.matmul_mx(
                    out=acc[:, w * HALF : (w + 1) * HALF], lhsT=v2_words[a][:, m].bitcast(FP8X4),
                    lhsT_scale=v2_sc[4 * a :, m], rhs=codes.bitcast(FP8X4), rhs_scale=sc,
                    start=(a == 0 and w == 0), stop=(a == PASSES - 1 and w == 1),
                )

        out_rows = out.rearrange("(i p) n -> p i n", p=P)

        def finish(acc, pair, u):
            th = e_tanh[:, 4 * u + pair, :]
            for w in range(2):
                n = slice(w * HALF, (w + 1) * HALF)
                nc.scalar.activation(th[:, n], acc[:, n], TANH, bias=bv_sb[:, 2 * pair + w : 2 * pair + w + 1])
            score = scores[:, 4 * u + pair, :]
            nc.vector.tensor_tensor(score, acc[:], th, MULT)
            nc.sync.dma_start(
                out_rows[:, 2 * pair : 2 * pair + 2, u * HALF : (u + 1) * HALF],
                score.rearrange("p (w n) -> p w n", w=2),
            )

        hs = [first_product(i) for i in range(H_SLOTS)]
        quantise_w1(1)
        for i in range(PASSES * PACK):
            scatter(i, hs[i], 2 if i == 0 else 1)
            if i + H_SLOTS < PASSES * PACK:
                hs.append(first_product(i + H_SLOTS))
            if i in (3, 4):
                gather(v2_words[i - 3][:], tab2_tiles[i - 3], lists["offs2"][:])

        x_all = held("x_all", [P, PASSES, PACK, HALF], F32, tag="h3")
        e_tanh = held("e_tanh", [P, BANKS, BANK], F32, tag="tab0")
        scores = held("scores", [P, BANKS, BANK], F32, tag="tab1")
        th_all = held("th_all", [P, PASSES, PACK, HALF], F32, tag="w1_raw0")
        accs = [[bank("e%d_%d" % (u, pair), 4 * u + pair) for pair in range(4)] for u in range(2)]

        def fetch_pass(a, u):
            for i in range(a * PACK, (a + 1) * PACK):
                fetch(i, x_all[:, a, :, :], th_all[:, a, :, :], u * HALF)

        def multiply(a, u, z):
            codes, sc = quantise_z("z%d_%d" % (a, u), z)
            for pair in range(4):
                second_pass(accs[u][pair], pair, a, codes[:], sc[:])

        for u in range(2):
            for a in range(PASSES):
                fetch_pass(a, u)
            zs = [
                rounder("z%d_%d" % (a, u), x_all[:, a, :, :], th_all[:, a, :, :])
                for a, rounder in enumerate((round_z_aside, round_z if u == 1 else round_z_aside))
            ]
            for a in range(PASSES):
                multiply(a, u, zs[a])
        for u in range(2):
            for pair in range(4):
                finish(accs[u][pair], pair, u)
